import numpy as np, ml_dtypes
CORES = [10,34,74,98]
N = 4
BF = ml_dtypes.bfloat16
def gentries(a):
    return np.ascontiguousarray(a.reshape(8, 16, -1).transpose(0, 2, 1)).reshape(8, -1)
def gtable(e):
    e = np.asarray(e); return np.ascontiguousarray(e.reshape(8, -1, 16).transpose(0, 2, 1)).reshape(128, -1).astype(np.int32)
V, E, LB, ST, RO = 4096, 1024, 10, 4, 3
def parts(rng):
    Q = 8 * N; q = np.arange(Q)[:, None]; k = np.arange(V)[None, :]
    o = np.argsort(rng.random((Q, V)), axis=1)
    x = np.zeros((Q, V, 16), np.float32); x[q, o] = np.linspace(235.0, 20.0, V)[None, :, None]
    x = x + rng.integers(4, 48, (Q, 1, 1)).astype(np.float32) * rng.standard_normal((Q, V, 16), dtype=np.float32)
    x = np.clip(np.floor(x), 0, 255)
    top = rng.integers(40, 700, (Q, 1)); nx = k + rng.integers(1, top + 1, (Q, V))
    nx = np.where((nx >= V) | (rng.random((Q, V)) < 0.015625), k, nx)
    S = np.zeros((Q, V), np.int64); S[q, o] = o[q, nx]
    pa = rng.integers(0, V, (Q, E)); far = np.where(rng.random((Q, E)) < 0.5, rng.integers(1, V, (Q, E)), rng.integers(1, 301, (Q, E)))
    a = o[q, pa]; b = o[q, (pa + far) % V]
    sa = S[q, a]; b = np.where((rng.random((Q, E)) < 0.0625) & (sa != a), sa, b)
    ix = np.where(rng.random((Q, E)) < 0.0625, rng.integers(0, E, (Q, E)), np.arange(E)[None, :])
    return x, S, a[q, ix], b[q, ix]
def pack(x, S, a, b):
    return {"x": np.ascontiguousarray(np.asarray(x).reshape(N, 8, V, 16).transpose(0, 1, 3, 2)).reshape(N, 128, V).astype(np.float32).astype(BF),
            "succ": np.ascontiguousarray(S.reshape(N, 8, V)).astype(np.int32),
            "ea": np.stack([gtable(e) for e in a.reshape(N, 8, E)]), "eb": np.stack([gtable(e) for e in b.reshape(N, 8, E)])}
def setup_inputs(rng):
    return pack(*parts(rng))
def setup_inputs_ties(rng):
    x, S, a, b = parts(rng); Q = 8 * N
    D = np.zeros((5, 16), np.int64); D[1, :8] = 1; D[1, 8:] = -1; D[2, :9] = 1; D[2, 9:] = -1; D[3, 0] = 1; D[4, 15] = -1
    A = rng.integers(1, 255, (Q, 1, 16)); A[3::8] = rng.choice(np.array([0, 255]), (N, 1, 16))
    y = np.clip(A + D[rng.integers(0, 5, (Q, V))], 0, 255)
    y[5::8] = A[5::8]; y[7::8] = x[7::8].astype(np.int64)
    for i in range(6, Q, 8):
        S[i] = np.where(S[i] % (V - 1) == 0, np.arange(V), S[i]); S[i, 0] = 0; S[i, V - 1] = V - 1
        hit = (a[i] % (V - 1) == 0) | (b[i] % (V - 1) == 0)
        a[i] = np.where(hit, 1, a[i]); b[i] = np.where(hit, 2, b[i])
        j = int(rng.integers(0, E)); a[i, j] = 0; b[i, j] = V - 1
        y[i, 0] = np.minimum(y[i, 0], 200); y[i, V - 1] = y[i, 0]; y[i, V - 1, int(rng.integers(0, 16))] += 50
    return pack(y, S, a, b)
def setup_inputs_crowd(rng):
    x, S, a, b = parts(rng); k = np.arange(E); v = np.arange(V)
    used = np.array(sorted({(ST * n + j) % LB for n in range(RO) for j in range(1, ST)}))
    hub = rng.permutation(V)
    for i in range(8 * N):
        g = i % 8; p = rng.permutation(V)
        if g in (0, 2, 4):
            d = (1, ST + 1, int(rng.choice(used)))[g // 2]; m = k & ~(1 << d)
            a[i] = p[2 * m]; b[i] = p[2 * m + 1]; S[i] = v
        elif g == 1:
            y = rng.permutation(E); j = np.arange(E - 257)
            a[i, y[:257]] = hub[0]; b[i, y[:257]] = hub[1]
            a[i, y[257:]] = hub[2 + 2 * j]; b[i, y[257:]] = hub[3 + 2 * j]
            S[i] = v; x[i] = np.minimum(x[i], 254); x[i, hub[0]] = 255
        elif g == 3:
            a[i] = p[rng.integers(0, 8, E)]; b[i] = p[8 + rng.integers(0, V - 8, E)]; x[i, p[:8]] = 255
        elif g == 5 and i // 8 == N - 1:
            a[i] = p[2 * k]; b[i] = p[2 * k + 1]; S[i] = v
        elif g == 5:
            n = V // 8
            if (i // 8) % 2 == 0: H = int(rng.integers(0, V - n + 1)) + np.arange(n)
            else: H = 8 * np.arange(n) + int(rng.integers(0, 8))
            z = rng.permutation(np.setdiff1d(v, H)); y = rng.permutation(E); j = np.arange(E - n)
            w = np.concatenate([z[:(ST - 1) * n].reshape(ST - 1, n), rng.permutation(H)[None, :]]); z = z[(ST - 1) * n:]
            S[i] = v; S[i, w[:-1]] = w[1:]
            x[i] = rng.integers(0, 128, (V, 16)); x[i, w] += 128
            a[i, y[:n]] = w[0]; b[i, y[:n]] = rng.permutation(z)[:n]
            a[i, y[n:]] = z[2 * j]; b[i, y[n:]] = z[2 * j + 1]
        elif g == 6:
            y = rng.permutation(k[((k >> 1) & 1) == 0]); c = np.concatenate([k[((k >> 1) & 1) == 1], y[:1]]); j = np.arange(E // 2 - 1)
            a[i, c] = hub[0]; b[i, c] = hub[1 + rng.permutation(E // 2 + 1)]
            a[i, y[1:]] = hub[E + 2 * j]; b[i, y[1:]] = hub[E + 2 * j + 1]
            S[i] = v; x[i] = np.minimum(x[i], 254); x[i, hub[0]] = 255
        else:
            m = np.where(((k >> 1) & 1) == 1, k & ~8, k)
            a[i] = p[2 * m]; b[i] = p[2 * m + 1]; S[i] = v
    return pack(x, S, a, b)
def setup_inputs_chains(rng):
    Q = 8 * N; q = np.arange(Q)[:, None]; k = np.arange(V)[None, :]
    C = rng.choice(np.array([2, 3, 4, 8, 16]), (Q, 1)); o = np.argsort(rng.random((Q, V)), axis=1)
    nx = k + C; nx = np.where(nx >= V, k, nx)
    S = np.zeros((Q, V), np.int64); S[q, o] = o[q, nx]
    x = np.zeros((Q, V, 16)); x[q, o] = np.floor(np.linspace(250.0, 1.0, V)[None, :, None] + 0.0625 * np.arange(16)[None, None, :])
    pa = rng.integers(0, V - 32, (Q, E)); pb = pa + rng.integers(1, C, (Q, E)); turn = rng.random((Q, E)) < 0.5
    return pack(x, S, o[q, np.where(turn, pb, pa)], o[q, np.where(turn, pa, pb)])
def setup_inputs_ends(rng):
    x, S, a, b = parts(rng); v = np.arange(V)
    x[0::2] = rng.choice(np.array([0.0, 255.0]), (4 * N, V, 16))
    S[0::8] = rng.integers(0, V, (N, V)); S[1::8] = 0; S[2::8] = V - 1; S[3::8] = V - 1 - v; S[4::8] = (v + 1) % V
    S[5::8] = v ^ 1; b[5::8] = a[5::8] ^ 1
    x[5::16] = rng.integers(0, 64, (N // 2, V, 16)) + 64 * (3 - v % 4)[None, :, None]
    S[5::16] = v - v % 4 + (v + 1) % 4; a[5::16] = 4 * rng.integers(0, V // 4, (N // 2, E)); b[5::16] = a[5::16] + 2
    w = 2 + rng.permutation(V - 4); M = V - 4 - 2 * ST
    for i in range(6, 8 * N, 8):
        S[i] = v; S[i, w[2 * ST:]] = rng.choice(w[2 * ST:], M)
        u = rng.integers(0, M, E); a[i] = w[2 * ST + u]; b[i] = w[2 * ST + (u + rng.integers(1, M, E)) % M]
        for c, (e, low) in enumerate(((0, 1), (V - 1, V - 2))):
            way = np.append(w[c * ST:(c + 1) * ST], e)
            S[i, way[:-1]] = way[1:]; x[i, way] = 255; x[i, low] = 0
        j = rng.permutation(E)[:2]
        a[i, j] = np.array([w[0], V - 2]); b[i, j] = np.array([1, w[ST]])
    a[7::8] = V - 1; b[7::8] = rng.integers(0, V - 1, (N, E))
    return pack(x, S, a, b)
def setup_inputs_spread(rng):
    Q = 8 * N
    x = np.minimum(np.floor(np.exp2(8 * rng.random((Q, V, 1))) * rng.random((Q, V, 16))), 255)
    S = rng.integers(0, V, (Q, V)); S = np.where(rng.random((Q, V)) < 0.0625, np.arange(V)[None, :], S)
    a = rng.integers(0, V, (Q, E)); b = (a + rng.integers(1, V, (Q, E))) % V
    return pack(x, S, a, b)
def check_inputs(d):
    bad = []; v = np.asarray(d["x"]).astype(np.float32)
    if not np.all((v >= 0) & (v <= 255) & (v == np.floor(v))): bad.append("x")
    for k in ("succ", "ea", "eb"):
        if np.min(d[k]) < 0 or np.max(d[k]) > V - 1: bad.append("range of " + k)
    if np.any(np.asarray(d["ea"]) == np.asarray(d["eb"])): bad.append("an edge with equal ends")
    return bad
def above(X, a, b):
    q = np.arange(X.shape[0])[:, None]
    m = np.add.reduce(np.sign(X[q, a] - X[q, b]), axis=2)
    return (m > 0) | ((m == 0) & (a < b))
def reference(x, succ, ea, eb):
    Q = 8 * N; q = np.arange(Q)[:, None]; lane = np.arange(E)[None, :]; qq = np.broadcast_to(q, (Q, E))
    X = np.ascontiguousarray(x.astype(np.float32).astype(np.int32).reshape(Q, 16, V).transpose(0, 2, 1))
    S = np.array(succ, np.int64).reshape(Q, V)
    fa = np.concatenate([gentries(e) for e in ea]).astype(np.int64); fb = np.concatenate([gentries(e) for e in eb]).astype(np.int64)
    a, b = fa, fb
    for rnd in range(RO):
        up = above(X, a, b); h = np.where(up, a, b); l = np.where(up, b, a)
        done = np.zeros((Q, E), bool); out = np.zeros((Q, E), bool)
        for k in range(ST):
            act = ~done & ~out
            s = S[q, h]
            met = act & (s == l)
            walk = act & ~met & (s != h) & above(X, s, l)
            ask = act & ~met & ~walk
            place = q * V + h
            n = np.bincount(place[ask], minlength=Q * V)[place]
            sole = ask & (n == 1); into = sole & (s != h)
            S[qq[sole], h[sole]] = l[sole]
            done = done | met | (sole & (s == h))
            h, l = np.where(into, l, np.where(walk, s, h)), np.where(into, s, l)
            out = ask & (n > 1) & (((lane >> ((rnd * ST + k + 1) % LB)) & 1) == 1)
        X = X + np.clip(X[q, S] - X, -1, 1)
        a = np.roll(np.where(done, fa, h), 8, axis=0); b = np.roll(np.where(done, fb, l), 8, axis=0)
        fa = np.roll(fa, 8, axis=0); fb = np.roll(fb, 8, axis=0)
    return {"ys": S.reshape(N, 8, V).astype(np.float32), "yx": np.ascontiguousarray(X.transpose(0, 2, 1)).reshape(N, 128, V).astype(np.float32).astype(BF)}

import numpy as np
from concourse.mybir import dt, AluOpType, ActivationFunctionType

AO = AluOpType
AF = ActivationFunctionType
ST_, RO, LB = 4, 3, 10
TR, SW = 4112, 4112 + 1024
PS = ["q%d" % i for i in range(8)]
SCRATCH = {"sdh": ("dram", [8, 4096], "bfloat16"), "sdl": ("dram", [8, 4096], "bfloat16"), "feat": ("dram", [4, 4096], "bfloat16")}
for _t, _names in (("bfloat16", "XA:4112 XB:4112 XC:4096 ID:4112 ST:5136 HW:1024 XL:1024 SG:1024 LW:1024 DD:1024 SN:1024 FG:1024 FW:256 "
                    "CF:512 CODE:512 GC:256 OHL:4096 OHH:4096 DX:4096 SX:4096 BS:2048 B1:2048 BP:2048 BW:2048 I1:128 I0:128 IK:128 "
                    "IN:128 IM:128 XS:256 ZB:256 ZZ:128 R1:64 R2:16 RV:32 BIT:128 SDB:512 FB:128 SLT:64 RTT:64 SLG:64 RTG:64"),
                   ("uint16", "LSU:256 HQ:64 LU:64 SU:64 SL:64 HL:64 FE0:128 FE1:128 FE2:128 PAY1:128 PAY2:128 ARR1:128 ARR2:128"),
                   ("int32", "EI:128 S128:256 SI:512 VI:128 CI:512 PI:16 JI:128 HI1:64 HI2:64 YI:64 ZI:64 BI:64"),
                   ("float32", "CFL:512 COL:64 YS:256 FA:128 J1:64 J2:64 h0:64 h1:64 l0:64 l1:64 om:64 dn0:64 dn1:64 wk:64 ask:64 "
                    "pwa:64 ob:64 om0:64 A0:64 m3:64 m4:64 m5:64 slf:64 hqf:64 va:64 vb:64 vc:64 vd:64 pc:64 pd:64")):
    for _e in _names.split():
        SCRATCH[_e.split(":")[0]] = ("sbuf", [128, int(_e.split(":")[1])], _t)
for _n in PS:
    SCRATCH[_n] = ("psum", [128, 512], "float32")
LOC = {"hw": ("q7", 0), "rt4": ("q7", 64), "dna": ("q7", 128), "dA": ("q7", 192), "TRF": ("q7", 256), "t1": ("q7", 320), "t2": ("q7", 384),
       "dlh": ("q7", 448), "dsl": ("q0", 128), "dsh": ("q0", 192), "dT": ("q0", 256), "met": ("q0", 320), "A1": ("q0", 384), "pb": ("q0", 448)}
SEMAPHORES = ["sV", "sA", "sP", "sG", "dx0", "dxc", "de", "dsu", "dsd", "dst", "dfe", "did", "dys", "dyx0", "dyx1", "dyx2", "dyx3",
              "rf1", "rf2", "rp1", "rp2", "loc"]


def make(g, T):
    eng = {"V": g.vector, "A": g.scalar, "P": g.tensor, "G": g, "S": g.sync}
    own = {"V": "sV", "A": "sA", "P": "sP", "G": "sG"}
    know = {e: {} for e in eng}
    total, snap, log = {}, {}, {}

    def need(e, reads, writes):
        w = {}
        for items, wr in ((reads, False), (writes, True)):
            for b, lo, hi in items:
                for e2, sem, val, lo2, hi2, wr2 in log.get(b, []):
                    if b in PS and e2 != e:
                        pass
                    elif e == "P" and e2 == e:
                        continue
                    elif hi <= lo2 or hi2 <= lo or not (wr or wr2):
                        continue
                    w[sem] = max(val, w.get(sem, 0))
        for sem, val in sorted(w.items(), key=lambda t: (-len(snap.get(t, {})), t)):
            if know[e].get(sem, 0) < val:
                eng[e].wait_ge(T.sem[sem], val)
                for s2, v2 in list(snap.get((sem, val), {}).items()) + [(sem, val)]:
                    know[e][s2] = max(v2, know[e].get(s2, 0))

    def note(e, tag, sem, val, reads, writes):
        snap[(sem, val)] = dict(know[e]) if e else {}
        for items, wr in ((reads, False), (writes, True)):
            for b, lo, hi in items:
                old = log.get(b, [])
                if b in PS and e == "P":
                    old = [r for r in old if r[0] != e]
                elif wr and b not in PS:
                    old = [r for r in old if not (lo <= r[3] and r[4] <= hi)]
                else:
                    old = [r for r in old if r[0] != tag or (r[5] and not wr) or not (lo <= r[3] and r[4] <= hi)]
                log[b] = old + [(tag, sem, val, lo, hi, wr)]

    def op(e, fn, reads, writes):
        need(e, reads, writes)
        sem = own[e]
        total[sem] = total.get(sem, 0) + 1
        fn(eng[e]).then_inc(T.sem[sem], 1)
        note(e, e, sem, total[sem], reads, writes)

    def dma(e, sem, pairs, reads, writes):
        need(e, reads, writes)
        for o, i in pairs:
            eng[e].dma_start(o, i).then_inc(T.sem[sem], 16)
        total[sem] = total.get(sem, 0) + 16 * len(pairs)
        note(e, "dma" + sem, sem, total[sem], reads, writes)

    def arrive(sem, val, writes):
        total[sem] = val
        note(None, "dma" + sem, sem, val, [], writes)

    return op, dma, need, arrive, total, know


def rank_program(g, core, T, topo):
    rank = T.rank_of(core)
    if rank is None:
        return
    N = len(T.cores)
    op, dma, need, arrive, total, know = make(g, T)

    def B(b, lo=0, hi=None):
        if b in LOC:
            q, o = LOC[b]
            return (T[q][:, o:o + 64], (q, o, o + 64))
        hi = SCRATCH[b][1][1] if hi is None else hi
        return (T[b][:, lo:hi], (b, lo, hi))

    def tt(out, a, b, o):
        op("V", lambda q: q.tensor_tensor(out[0], a[0], b[0], o), [a[1], b[1]], [out[1]])

    def ts(out, a, s1, s2, o0, o1=None, extra=()):
        if o1 is None:
            op("V", lambda q: q.tensor_scalar(out[0], a[0], s1, None, o0), [a[1]] + list(extra), [out[1]])
        else:
            op("V", lambda q: q.tensor_scalar(out[0], a[0], s1, s2, o0, o1), [a[1]] + list(extra), [out[1]])

    def tc(out, a):
        op("V", lambda q: q.tensor_copy(out[0], a[0]), [a[1]], [out[1]])

    def act(out, a, f):
        op("A", lambda q: q.activation(out[0], a[0], f), [a[1]], [out[1]])

    def clamp(out, a):
        ts(out, a, 1.0, -1.0, AO.min, AO.max)

    def fill(b, lo, hi, c):
        op("V", lambda q: q.memset(T[b][:, lo:hi], c), [], [(b, lo, hi)])

    def mm(out, ok, lhs, rhs, keys, start, stop):
        op("P", lambda q: q.matmul(out, lhs, rhs, start, stop), keys, [ok])

    def gather(e, out, win, lst, c0, c1):
        src = T[win][:, 0:256 if win == "FW" else TR].indirect(T[lst][:, c0:c1])
        rd = [(win, 0, TR), (lst, c0, c1)]
        if e == "A":
            op("A", lambda q: q.activation(out[0], src, AF.Copy), rd, [out[1]])
        else:
            op("V", lambda q: q.tensor_copy(out[0], src), rd, [out[1]])

    def gsub(out, win, lst, c0, c1, less):
        op("V", lambda q: q.tensor_tensor(out[0], T[win][:, 0:TR].indirect(T[lst][:, c0:c1]), less[0], AO.subtract),
           [(win, 0, TR), (lst, c0, c1), less[1]], [out[1]])

    def send(nm, src, d, sem):
        dst, frm = T.cores[(rank + d) % N], T.cores[(rank - d) % N]
        rid, pid, _s = topo.addr(dst)
        need("G", [(src, 0, 128)], [])
        g.remote_dma(T[nm][:], T[src][:], T.sem[sem], T.sem.loc, pid, rid, topo.mask(core, dst))
        total["loc"] = total.get("loc", 0) + len(topo.engines(core, dst))
        arrive(sem, len(topo.engines(frm, core)), [(nm, 0, 128)])

    def wide_to_g(dst, c0, bnm, src, start, stop):
        for i in range(16):
            mm(T[dst][:, c0:c0 + 64], (dst, c0, c0 + 64), T[bnm][:, 128 * i:128 * i + 128], T[src][:, i:1024:16],
               [(bnm, 128 * i, 128 * i + 128), (src, 0, 1024)], start and i == 0, stop and i == 15)

    def col(c):
        return T.COL[:, c:c + 1], ("COL", c, c + 1)

    dma("S", "de", [(T.EI[:, 0:64], T.ea[:, :]), (T.EI[:, 64:128], T.eb[:, :])], [], [("EI", 0, 128)])
    dma("A", "dsu", [(T.S128[:], T.succ[:, :])], [], [("S128", 0, 256)])
    dma("S", "dx0", [(T.XA[:, 0:4096], T.x[:, :])], [], [("XA", 0, 4096)])
    op("G", lambda q: q.iota(T.PI[:, 0:1], [[0, 1]], 0, 1), [], [("PI", 0, 1)])
    op("G", lambda q: q.iota(T.VI[:, 0:32], [[1, 32]], 0, 32), [], [("VI", 0, 32)])
    op("G", lambda q: q.iota(T.CI[:, 0:128], [[1, 128]], 0, 0), [], [("CI", 0, 128)])
    op("G", lambda q: q.iota(T.JI[:, 0:64], [[16, 64]], 0, 0), [], [("JI", 0, 64)])
    op("G", lambda q: q.iota(T.ST[:], [[0, SW]], 0, 0, allow_small_or_imprecise_dtypes=True), [], [("ST", 0, SW)])
    ts(B("VI", 32, 64), B("VI", 0, 32), 6, None, AO.logical_shift_right)
    ts(B("VI", 64, 96), B("VI", 0, 32), 63, None, AO.bitwise_and)
    tc(B("FB", 0, 64), B("VI", 32, 96))
    fill("FB", 64, 96, 1.0)
    ts(B("PI", 1, 2), B("PI", 0, 1), 4, None, AO.logical_shift_right)
    ts(B("PI", 2, 3), B("PI", 0, 1), 15, None, AO.bitwise_and)
    ts(B("PI", 4, 5), B("PI", 0, 1), 3, None, AO.logical_shift_right)

    def pow2(dst, srccol, sign):
        for k in range(4):
            ts(B("PI", 8 + k, 9 + k), B("PI", srccol, srccol + 1), k, 1, AO.logical_shift_right, AO.bitwise_and)
        for k in range(4):
            ts(B("COL", 60 + k, 61 + k), B("PI", 8 + k, 9 + k), 2.0 ** (sign * (1 << k)) - 1.0, 1.0, AO.mult, AO.add)
        tt(B("COL", dst, dst + 1), B("COL", 60, 61), B("COL", 61, 62), AO.mult)
        tt(B("COL", 62, 63), B("COL", 62, 63), B("COL", 63, 64), AO.mult)
        tt(B("COL", dst, dst + 1), B("COL", dst, dst + 1), B("COL", 62, 63), AO.mult)

    pow2(20, 4, -1)
    fill("FB", 96, 128, 32768.0)
    ts(B("FB", 96, 128), B("FB", 96, 128), col(20)[0], None, AO.mult, None, [col(20)[1]])
    dma("S", "dfe", [(T.feat[f:f + 1, :], T.FB[:, 32 * f:32 * f + 32]) for f in range(4)], [("FB", 0, 128)], [("feat", 0, 1)])
    tc(B("COL", 0, 3), B("PI", 0, 3))
    ts(B("CI", 128, 256), B("CI", 0, 128), 4, None, AO.logical_shift_right)
    ts(B("CI", 256, 384), B("CI", 0, 128), 15, None, AO.bitwise_and)
    tc(B("CFL", 0, 384), B("CI", 0, 384))
    ts(B("CFL", 384, 512), B("CFL", 128, 256), col(1)[0], None, AO.is_equal, None, [col(1)[1]])
    ts(B("CFL", 256, 384), B("CFL", 256, 384), 1.0, None, AO.add)
    tt(B("ZZ"), B("CFL", 256, 384), B("CFL", 384, 512), AO.mult)
    for i in range(16):
        ts(B("B1", 128 * i, 128 * i + 128), B("ZZ"), float(i + 1), None, AO.is_equal)
    ts(B("I1"), B("CFL", 0, 128), col(0)[0], None, AO.is_equal, None, [col(0)[1]])
    for k in range(4):
        ts(B("COL", 4 + k, 5 + k), B("COL", 2, 3), float(k), None, AO.is_equal)
    pow2(10, 2, 1)
    ts(B("COL", 8, 9), B("COL", 4, 5), 64.0, None, AO.mult)
    tt(B("COL", 8, 9), B("COL", 8, 9), B("COL", 5, 6), AO.add)
    for nm, c in (("BS", 8), ("BP", 7), ("BW", 10)):
        op("A", lambda q: q.activation(T[nm][:], T.B1[:], AF.Copy, scale=col(c)[0]), [("B1", 0, 2048), col(c)[1]], [(nm, 0, 2048)])
    fill("ID", 0, TR, 0.0)
    dma("S", "did", [(T.ID[16 * q:16 * q + 4, 0:4096], T.feat[:, :]) for q in range(8)], [("feat", 0, 1)], [("ID", 0, 4096)])
    ts(B("SI", 0, 256), B("S128"), 6, None, AO.logical_shift_right)
    ts(B("SI", 256, 512), B("S128"), 63, None, AO.bitwise_and)
    tc(B("SDB"), B("SI"))
    dma("S", "dsd", [(T.sdh[:, :], T.SDB[:, 0:256]), (T.sdl[:, :], T.SDB[:, 256:512])], [("SDB", 0, 512)], [("sdh", 0, 1)])
    tc(B("FE0"), B("EI"))
    dma("S", "dst", [(T.ST[0:128:16, 0:4096], T.sdh[:, :]), (T.ST[1:128:16, 0:4096], T.sdl[:, :])], [("sdh", 0, 1)], [("ST", 0, 4096)])
    fill("XA", 4096, TR, 0.0)
    fill("XB", 4096, TR, 0.0)
    ts(B("COL", 58, 59), B("COL", 4, 5), -1000.0, None, AO.mult)
    tt(B("COL", 58, 59), B("COL", 58, 59), B("COL", 6, 7), AO.add)
    ts(B("ID", 4096, TR), B("ID", 4096, TR), col(58)[0], None, AO.add, None, [col(58)[1]])
    ts(B("COL", 57, 58), B("COL", 4, 5), 64.0, None, AO.mult)
    ts(B("ST", 4096, TR), B("ST", 4096, TR), col(57)[0], None, AO.add, None, [col(57)[1]])

    def sel(nm, n0, n1, g0, c):
        ts(B(nm, n0, n1), B("CFL", g0, g0 + n1 - n0), col(1)[0], col(c)[0], AO.is_equal, AO.mult, [col(1)[1], col(c)[1]])

    for r in range(4):
        ts(B("COL", 48 + r, 49 + r), B("COL", 6, 7), float(3 - r), None, AO.mult)
    for r in range(4):
        tt(B("COL", 12 + r, 13 + r), B("COL", 48 + r, 49 + r), B("COL", 5, 6), AO.add)
        tt(B("COL", 16 + r, 17 + r), B("COL", 48 + r, 49 + r), B("COL", 4, 5), AO.add)
    for r in range(4):
        sel("R1", 8 * r, 8 * r + 8, 0, 12 + r)
        for hf in range(2):
            sel("R1", 32 + hf * 16 + r * 4, 36 + hf * 16 + r * 4, 4 * hf, 16 + r)
    fill("ZB", 0, 256, 0.0)
    dma("S", "dxc", [(T.XC[:], T.x[:, :])], [], [("XC", 0, 4096)])

    def rest_of_constants():
        ts(B("COL", 9, 10), B("COL", 8, 9), -1.0, None, AO.mult)
        fill("COL", 25, 26, 1024.0)
        for nm, f in (("I0", -1.0), ("IK", 1024.0), ("IN", -131072.0), ("IM", -128.0)):
            ts(B(nm), B("I1"), f, None, AO.mult)
        for n0, c in ((0, 8), (8, 9)):
            sel("R2", n0, n0 + 8, 0, c)
        for r in range(4):
            for hf in range(2):
                sel("RV", hf * 16 + r * 4, hf * 16 + r * 4 + 4, 4 * hf, 25)
        tc(B("J1"), B("JI", 0, 64))
        ts(B("J2"), B("J1"), col(2)[0], None, AO.add, None, [col(2)[1]])
        tc(B("JI", 64, 128), B("J2"))
        ts(B("TRF"), B("J2"), float(TR), None, AO.add)
        tc(B("FA"), B("EI"))
        bit(1)

    def bit(t):
        ts(B("BI"), B("JI", 64, 128), t % LB, 1, AO.logical_shift_right, AO.bitwise_and)
        tc(B("BIT", 64 * (t % 2), 64 * (t % 2) + 64), B("BI"))

    cur, nxt = "XA", "XB"
    for n in range(RO):
        fe, ar = ("FE0", "FE0") if n == 0 else ("FE%d" % n, "ARR%d" % n)
        for q in range(4):
            gather("A", B("XL", 256 * q, 256 * q + 256), cur, ar, 64 + 16 * q, 80 + 16 * q)
        tc(B("va"), B(ar, 0, 64))
        tc(B("vb"), B(ar, 64, 128))
        tt(B("vc"), B("va"), B("vb"), AO.subtract)
        ts(B("SLG"), B("vc"), 0.0, None, AO.is_lt)
        for q in range(4):
            c0, c1 = 256 * q, 256 * q + 256
            gsub(B("DD", c0, c1), cur, ar, 16 * q, 16 * q + 16, B("XL", c0, c1))
            if q < 2:
                act(B("SN", c0, c1), B("DD", c0, c1), AF.Sign)
        clamp(B("SN", 512, 1024), B("DD", 512, 1024))
        if n == 0:
            rest_of_constants()
            send("FE1", "FE0", 1, "rf1")
            send("FE2", "FE0", 2, "rf2")
        mm(T.q4[:, 0:64], ("q4", 0, 64), T.I1[:], T.SLG[:], [("I1", 0, 128), ("SLG", 0, 64)], True, False)
        wide_to_g("q4", 0, "B1", "SN", False, True)
        ts(B("wk"), B("q4", 0, 64), 0.0, None, AO.is_gt)
        tt(B("vd"), B("wk"), B("vc"), AO.mult)
        h, l, h2, l2, dn, dn2 = "h0", "l0", "h1", "l1", "dn0", "dn1"
        tt(B(h), B("vb"), B("vd"), AO.add)
        tc(B("HQ"), B(h))
        tt(B(l), B("va"), B("vd"), AO.subtract)
        tc(B("LU"), B(l))
        deferred = []
        for k in range(ST_):
            t = ST_ * n + k
            first, last = k == 0, k == ST_ - 1

            def low_digits(u0, u1):
                for u in range(u0, u1):
                    ts(B("OHL", 256 * u, 256 * u + 256), B("CODE", 0, 256), float(4 * u + 3), None, AO.is_equal)

            gather("A", B("HW"), "ID", "HQ", 0, 64)
            if first:
                gather("V", B("SG"), "ST", "HQ", 0, 64)
                wide_to_g("q0", 0, "BS", "SG", True, True)
            for b in range(8):
                mm(T.q1[:, b:512:8], ("q1", 0, 512), T.HW[:, 128 * b:128 * b + 128], T.R1[:], [("HW", 0, 1024), ("R1", 0, 64)], True, True)
            if first:
                gather("A", B("XL", 0, 512), cur, "LU", 0, 32)
                gather("V", B("XL", 512, 1024), cur, "LU", 32, 64)
                act(B("CODE"), B("q1"), AF.Copy)
            else:
                gather("A", B("XL"), cur, "LU", 0, 64)
                act(B("CODE"), B("q1"), AF.Copy)
                gather("A", B("SG"), "ST", "HQ", 0, 64)
            gather("A", B("LW"), "ID", "LU", 0, 64)
            if not first:
                wide_to_g("q0", 64, "BP", "HW", True, True)
            mm(T.q3[:, 0:256], ("q3", 0, 256), T.ZB[:, 0:128], T.ZB[:, 0:256], [("ZB", 0, 256)], True, False)
            if first:
                fill(dn, 0, 64, 0.0)
                fill("om", 0, 64, 0.0)
                wide_to_g("q0", 64, "BP", "HW", True, True)
            else:
                low_digits(0, 16)
                for f in deferred:
                    f()
                deferred = []
                wide_to_g("q0", 0, "BS", "SG", True, True)
            tc(B("SU"), B("q0", 0, 64))
            for qn, o, src2 in (("q6", 64, "HW"), ("q2", 0, "LW")):
                for b in range(8):
                    for j, src in enumerate(("SG", src2)):
                        mm(T[qn][:, o + b:o + 64:8], (qn, o, o + 64), T[src][:, 128 * b:128 * b + 128], T.R2[:, 8 * j:8 * j + 8],
                           [(src, 0, 1024), ("R2", 0, 16)], j == 0, j == 1)
            for q in range(3):
                c0, c1 = 256 * q, 256 * q + 256
                gsub(B("DD", c0, c1), cur, "SU", 16 * q, 16 * q + 16, B("XL", c0, c1))
            gather("A", B("XS"), cur, "SU", 48, 64)
            mm(T.q5[:, 0:256], ("q5", 0, 256), T.I0[:], T.XL[:, 768:1024], [("I0", 0, 128), ("XL", 768, 1024)], True, False)
            mm(T.q5[:, 0:256], ("q5", 0, 256), T.I1[:], T.XS[:], [("I1", 0, 128), ("XS", 0, 256)], False, True)
            for q in (0, 1):
                act(B("SN", 256 * q, 256 * q + 256), B("DD", 256 * q, 256 * q + 256), AF.Sign)
            act(B("SN", 768, 1024), B("q5", 0, 256), AF.Sign)
            clamp(B("SN", 512, 768), B("DD", 512, 768))
            if first:
                low_digits(0, 8)
            ts(B("RTT"), B("q6", 64, 128), 0.0, None, AO.is_equal)
            ts(B("SLT"), B("q2", 0, 64), 0.0, None, AO.is_le)
            for nm, w in (("RTT", "IN"), ("SLT", "IK")):
                for hf in range(2):
                    for r in range(4):
                        o = hf * 128 + r * 32
                        mm(T.q3[:, o:o + 32], ("q3", 0, 256), T[w][:], T[nm][:, hf * 32:hf * 32 + 32], [(w, 0, 128), (nm, 0, 64)], False, False)
            for b in range(8):
                c0 = 256 * (b // 2)
                mm(T.q3[:, b:256:8], ("q3", 0, 256), T.SN[:, 128 * b:128 * b + 128], T.RV[:], [("SN", c0, c0 + 256), ("RV", 0, 32)], False, b == 7)
            tt(B("dsl"), B("q0", 0, 64), B(l), AO.subtract)
            tt(B("dsh"), B("q0", 0, 64), B(h), AO.subtract)
            ts(B("SLG"), B("dsl"), 0.0, None, AO.is_le)
            ts(B("RTG"), B("dsh"), 0.0, None, AO.is_equal)
            mm(T.q4[:, 0:64], ("q4", 0, 64), T.I1[:], T.SLG[:], [("I1", 0, 128), ("SLG", 0, 64)], True, False)
            mm(T.q4[:, 0:64], ("q4", 0, 64), T.IM[:], T.RTG[:], [("IM", 0, 128), ("RTG", 0, 64)], False, False)
            wide_to_g("q4", 0, "B1", "SN", False, True)
            if first:
                low_digits(8, 16)
            ts(B("rt4"), B("dsh"), 0.0, 4096.0, AO.is_equal, AO.mult)
            ts(B("met"), B("dsl"), 0.0, 4096.0, AO.is_equal, AO.mult)
            tc(B("HI1"), B("HQ"))
            tt(B("dT"), B(h), B("TRF"), AO.subtract)
            tt(B("A1"), B(l), B("rt4"), AO.max)
            ts(B("HI2"), B("HI1"), 255, None, AO.bitwise_and)
            tt(B("dna"), B(dn), B("met"), AO.max)
            tc(B("HL"), B("HI2"))
            for hf in range(2):
                tt(B("GC", 128 * hf, 128 * hf + 128), B("q3", 128 * hf, 128 * hf + 128), B("CODE", 256 + 128 * hf, 384 + 128 * hf), AO.max)
                for u in range(16):
                    o = hf * 2048 + u * 128
                    ts(B("OHH", o, o + 128), B("GC", 128 * hf, 128 * hf + 128), float(4 * u + 3), None, AO.is_equal)
                qn = "q5" if hf == 0 else "q6"
                for g4 in range(4):
                    for b in range(8):
                        c = (4 * hf + g4) * 8 + b
                        mm(T[qn][0:64, 64 * g4:64 * g4 + 64], (qn, 0, 256), T.OHL[:, c:4096:64],
                           T.OHH[:, hf * 2048 + g4 * 8 + b:(hf + 1) * 2048:32], [("OHL", 0, 4096), ("OHH", hf * 2048, hf * 2048 + 2048)], b == 0, b == 7)
            ts(B("ask"), B("q4", 0, 64), 0.0, None, AO.is_le)
            tt(B("wk"), B("q4", 0, 64), B("om"), AO.is_gt)
            op("V", lambda v: v.tensor_scalar(T.CF[0:64, 0:256], T.q5[0:64, 0:256], 1.0, None, AO.is_equal), [("q5", 0, 256)], [("CF", 0, 256)])
            tt(B("pwa"), B("q0", 64, 128), B("ask"), AO.mult)
            tt(B("t2"), B("wk"), B("dsh"), AO.mult)
            if not last:
                z = 64 * ((t + 1) % 2)
                ts(B("t1"), B("pwa"), 0.0, 4096.0, AO.is_gt, AO.mult)
            tt(B("hw"), B(h), B("t2"), AO.add)
            if not last:
                tt(B("ob"), B("BIT", z, z + 64), B("t1"), AO.mult)
                tt(B("dlh"), B(l), B("hw"), AO.subtract)
                tt(B("om0"), B("ob"), B("dna"), AO.max)
            else:
                tt(B("dlh"), B(l), B("hw"), AO.subtract)
            op("V", lambda v: v.tensor_scalar(T.CF[0:64, 256:512], T.q6[0:64, 0:256], 1.0, None, AO.is_equal), [("q6", 0, 256)], [("CF", 256, 512)])
            for s in range(4):
                qn, o = ("q2", 128 + 64 * s) if s < 2 else ("q3", 256 + 64 * (s - 2))
                mm(T[qn][:, o:o + 64], (qn, o, o + 64), T.CF[0:64, s:512:4], T.I1[0:64, 0:64], [("CF", 0, 512), ("I1", 0, 128)], True, True)
            if not last:
                tt(B("A0"), B("om0"), B("hw"), AO.max)
            act(B("FW", 0, 128), B("q2", 128, 256), AF.Copy)
            tc(B("FW", 128, 256), B("q3", 256, 384))
            gather("A", B("FG", 512, 1024), "FW", "HL", 32, 64)
            gather("V", B("FG", 0, 512), "FW", "HL", 0, 32)
            wide_to_g("q4", 64, "BW", "FG", True, True)
            if not last:
                tt(B("dA"), B("A1"), B("A0"), AO.subtract)
            if t + 2 < ST_ * RO:
                bit(t + 2)
            tt(B("YI"), B("q4", 64, 128), B("pwa"), AO.mult)
            ts(B("ZI"), B("YI"), 15, 1, AO.logical_shift_right, AO.bitwise_and)
            tt(B("m3"), B("ZI"), B("dT"), AO.mult)
            if not last:
                tt(B("t2"), B("ZI"), B("dsl"), AO.mult)
                tt(B("t1"), B("ZI"), B("dA"), AO.mult)
                tt(B("slf"), B("m3"), B("TRF"), AO.add)
                tt(B(l2), B(l), B("t2"), AO.add)
                tt(B("hqf"), B("A0"), B("t1"), AO.add)
                tc(B("SL"), B("slf"))
                tc(B("LU"), B(l2))
                tc(B("HQ"), B("hqf"))
            elif n < RO - 1:
                tt(B("t2"), B("ZI"), B("dsl"), AO.mult)
                tt(B("m4"), B("ZI"), B("dlh"), AO.mult)
                tt(B("m5"), B("ZI"), B("rt4"), AO.mult)
                tt(B("slf"), B("m3"), B("TRF"), AO.add)
                tt(B("t2"), B(l), B("t2"), AO.add)
                tt(B("t1"), B("m4"), B("hw"), AO.add)
                tt(B(dn2), B("m5"), B("dna"), AO.max)
                tc(B("SL"), B("slf"))
                ts(B(dn2), B(dn2), 1.0 / 4096.0, None, AO.mult)
                if n > 0:
                    tc(B("FA"), B(fe))
                tt(B("dsh"), B("FA", 0, 64), B("t1"), AO.subtract)
                tt(B("pb"), B("FA", 64, 128), B("t2"), AO.subtract)
                tt(B("pc"), B(dn2), B("dsh"), AO.mult)
                tt(B("pd"), B(dn2), B("pb"), AO.mult)
                tt(B("pc"), B("pc"), B("t1"), AO.add)
                tt(B("pd"), B("pd"), B("t2"), AO.add)
                py = "PAY%d" % (n + 1)
                tc(B(py, 0, 64), B("pc"))
                tc(B(py, 64, 128), B("pd"))
                send("ARR%d" % (n + 1), py, 1, "rp%d" % (n + 1))
            else:
                tt(B("slf"), B("m3"), B("TRF"), AO.add)
                tc(B("SL"), B("slf"))
            op("V", lambda v: v.tensor_copy(T.ST[:, 0:SW].indirect(T.SL[:, 0:64]), T.LW[:, 0:1024]), [("LW", 0, 1024), ("SL", 0, 64)], [("ST", 0, SW)])

            def state(h2=h2, dn2=dn2):
                tt(B("m4"), B("ZI"), B("dlh"), AO.mult)
                tt(B("m5"), B("ZI"), B("rt4"), AO.mult)
                ts(B("om"), B("hqf"), 4096.0, 4096.0, AO.is_ge, AO.mult)
                tt(B(h2), B("m4"), B("hw"), AO.add)
                tt(B(dn2), B("m5"), B("dna"), AO.max)
            if not last:
                deferred.append(state)
                h, h2, l, l2, dn, dn2 = h2, h, l2, l, dn2, dn
        bank = ("q5", "q6", "q4", "q7")
        for q in range(4):
            for i in range(16):
                mm(T[bank[q]][:, 64 * q:64 * q + 64], (bank[q], 0, 256), T.BS[:, 128 * i:128 * i + 128], T.ST[:, 1024 * q + i:1024 * q + 1024:16],
                   [("BS", 0, 2048), ("ST", 0, TR)], i == 0, i == 15)

        def finish(c):
            qn = ("q0", "q1", "q2", "q3")[c % 4]
            c0, c1 = 512 * c, 512 * c + 512
            mm(T[qn][:], (qn, 0, 512), T.I1[:], T[cur][:, c0:c1], [("I1", 0, 128), (cur, c0, c1)], True, False)
            mm(T[qn][:], (qn, 0, 512), T.I1[:], T.SX[:, c0:c1], [("I1", 0, 128), ("SX", c0, c1)], False, True)
            act(B(nxt, c0, c1), B(qn), AF.Copy)

        for c in range(8):
            c0, c1 = 512 * c, 512 * c + 512
            if c % 2 == 0:
                q = c // 2
                tc(B("LSU", 64 * q, 64 * q + 64), B(bank[q], 64 * q, 64 * q + 64))
            gsub(B("DX", c0, c1), cur, "LSU", 32 * c, 32 * c + 32, B("XC", c0, c1))
            if c in (2, 4, 6, 7):
                clamp(B("SX", c0, c1), B("DX", c0, c1))
            else:
                act(B("SX", c0, c1), B("DX", c0, c1), AF.Sign)
            if c > 0:
                finish(c - 1)
            if n == RO - 1 and c == 2:
                for i in range(16):
                    mm(T.q5[:, 0:256], ("q5", 0, 256), T.BS[:, 128 * i:128 * i + 128], T.ST[:, 256 * i:256 * i + 256], [("BS", 0, 2048), ("ST", 0, TR)], i == 0, i == 15)
                tc(B("YS"), B("q5", 0, 256))
                dma("S", "dys", [(T.ys[:, :], T.YS[:])], [("YS", 0, 256)], [])
            if n == RO - 1 and c in (2, 4, 6):
                d = c // 2 - 1
                dma("S", "dyx%d" % d, [(T.yx[:, 1024 * d:1024 * d + 1024], T[nxt][:, 1024 * d:1024 * d + 1024])], [(nxt, 1024 * d, 1024 * d + 1024)], [])
        finish(7)
        if n == RO - 1:
            dma("S", "dyx3", [(T.yx[:, 3072:4096], T[nxt][:, 3072:4096])], [(nxt, 3072, 4096)], [])
        cur, nxt = nxt, cur
        if n < RO - 1:
            dma("S", "dxc", [(T.XC[:], T[cur][:, 0:4096])], [(cur, 0, 4096)], [("XC", 0, 4096)])
    for sem, val in total.items():
        if know["G"].get(sem, 0) < val:
            g.wait_ge(T.sem[sem], val)
